import numpy as np
import ml_dtypes


def mxq(x, axis, fmt="e4m3"):
    dtype, down = {"e4m3": (ml_dtypes.float8_e4m3fn, 7), "e5m2": (ml_dtypes.float8_e5m2, 14)}[fmt]
    v = np.moveaxis(np.asarray(x, np.float32).astype(ml_dtypes.bfloat16).astype(np.float64), axis, -1)
    blocks = v.reshape(v.shape[:-1] + (-1, 32))
    amax = np.abs(blocks).max(-1, keepdims=True)
    byte = np.maximum(np.where(amax > 0, np.frexp(amax)[1] - 1 + 127, 0) - down, 1)
    scale = np.exp2(byte - 127.0)
    codes = (blocks / scale).astype(np.float32).astype(dtype).astype(np.float64)
    return np.moveaxis((codes * scale).reshape(v.shape), -1, axis)


WIDE = False


def mx_kscale(k):
    if not WIDE:
        return np.ones(k)
    levels = np.array([10, -10, 5, -5, 0])
    if k % 512:
        return np.exp2(np.random.permutation(np.resize(levels, k // 32))).repeat(32)
    a = np.empty((k // 512, 16))
    for p in range(k // 512):
        a[p, :8] = np.random.permutation(np.resize(levels, 8))
        for g in range(8):
            far = levels[np.abs(levels - a[p, g]) >= 10]
            a[p, g + 8] = far[np.random.randint(len(far))]
    return np.exp2(a.ravel()).repeat(32)


def f64(x):
    return np.asarray(x).astype(np.float64)


def striped(idx):
    return np.tile(idx.reshape(-1, 16).T, (8, 1)).astype(np.uint16)


def unstriped(offs):
    return offs[:16].T.reshape(-1).astype(np.int64)


def striped8(idx):
    return np.concatenate([x.reshape(-1, 16).T for x in idx]).astype(np.uint16)


def runs(offs, k):
    lists = np.stack([offs[16 * r : 16 * r + 16].T.reshape(-1) for r in range(8)]).astype(np.int64)
    return lists[np.arange(k) % 512 // 64]


def pack_weight(w):
    k, n = w.shape
    w = f64(np.asarray(w, np.float32).astype(ml_dtypes.bfloat16)).reshape(k // 32, 32, n)
    amax = np.abs(w).max(1)
    byte = np.clip(np.where(amax > 0, np.frexp(amax)[1] - 1 + 127 - 7, 1), 1, 254)
    scaled = (w * np.exp2(127.0 - byte)[:, None, :]).reshape(k, n).astype(np.float32)
    words = np.ascontiguousarray(scaled.reshape(k // 512, 128, 4, n).transpose(0, 1, 3, 2)).astype(ml_dtypes.float8_e4m3fn).view(np.uint8)
    return words, np.ascontiguousarray(byte.astype(np.uint8).reshape(k // 512, 16, n))


def unpack_weight(words, scales):
    g, p, n, _ = words.shape
    vals = np.ascontiguousarray(words).view(ml_dtypes.float8_e4m3fn).astype(np.float64) * np.repeat(np.exp2(scales.astype(np.float64) - 127.0), 8, axis=1)[..., None]
    return vals.transpose(0, 1, 3, 2).reshape(g * 512, n)


E2M1 = np.array([0.0, 0.5, 1.0, 1.5, 2.0, 3.0, 4.0, 6.0, -0.0, -0.5, -1.0, -1.5, -2.0, -3.0, -4.0, -6.0])


def pack_fp4(w):
    k, n = w.shape
    w = f64(np.asarray(w, np.float32).astype(ml_dtypes.bfloat16)).reshape(k // 32, 32, n)
    amax = np.abs(w).max(1)
    mant, ex = np.frexp(amax / 6.0)
    byte = np.clip(np.where(amax > 0, np.where(mant > 0.5, ex, ex - 1) + 127, 1), 1, 254)
    scaled = (w * np.exp2(127.0 - byte)[:, None, :]).reshape(k, n).astype(np.float32)
    c = np.ascontiguousarray(scaled.reshape(k // 512, 128, 4, n).transpose(0, 1, 3, 2)).astype(ml_dtypes.float4_e2m1fn).view(np.uint8) & 0xF
    words = (c[..., 0::2] | (c[..., 1::2] << 4)).reshape(k // 512, 128, 2 * n)
    return np.ascontiguousarray(words), np.ascontiguousarray(byte.astype(np.uint8).reshape(k // 512, 16, n))


def unpack_fp4(words, scales):
    g, _, n = scales.shape
    words = np.ascontiguousarray(words).reshape(g, 128, n, 2)
    nib = np.empty((g, 128, n, 4), np.uint8)
    nib[..., 0::2] = words & 0xF
    nib[..., 1::2] = words >> 4
    vals = E2M1[nib] * np.repeat(np.exp2(scales.astype(np.float64) - 127.0), 8, axis=1)[..., None]
    return vals.transpose(0, 1, 3, 2).reshape(g * 512, n)


def sigmoid(v):
    return 1.0 / (1.0 + np.exp(-np.maximum(v, -700.0)))

def planes(y):
    n, m = y.shape
    v = y.astype(np.float32).astype(ml_dtypes.bfloat16).astype(np.float64).reshape(n // 32, 32, m)
    top = np.abs(v).max(1)
    byte = np.clip(np.where(top > 0, np.frexp(top)[1] - 1 + 127 - 7, 1), 1, 254)
    codes = (v * np.exp2(127.0 - byte)[:, None, :]).reshape(n, m).astype(np.float32).astype(ml_dtypes.float8_e4m3fn).view(np.uint8)
    words = codes.reshape(n // 512, 128, 4, m).transpose(0, 1, 3, 2)
    return np.ascontiguousarray(words), np.ascontiguousarray(byte.astype(np.uint8).reshape(n // 512, 16, m))


K, T, S, V, H, J = 512, 2048, 512, 256, 512, 512


def setup_inputs():
    n = np.random.standard_normal
    s = mx_kscale(K)[:, None]
    u = mx_kscale(S)
    packed_xT = pack_weight(n((K, T)) * s)
    packed_w1 = pack_fp4(n((K, H)) / np.sqrt(K) / s)
    packed_w2 = pack_fp4(n((K, H)) / np.sqrt(K) / s)
    packed_w3 = pack_fp4(n((K, H)) / np.sqrt(K) / s)
    return {
        "x_words": packed_xT[0],
        "x_scales": packed_xT[1],
        "w1_words": packed_w1[0],
        "w1_scales": packed_w1[1],
        "w2_words": packed_w2[0],
        "w2_scales": packed_w2[1],
        "w3_words": packed_w3[0],
        "w3_scales": packed_w3[1],
        "ga": (np.random.uniform(0.5, 1.5, (H, 1)) * u[:, None]).astype(np.float32),
        "gb": (np.random.uniform(0.5, 1.5, (H, 1)) / u[:, None]).astype(np.float32),
        "tab": n((S, J)).astype(np.float32),
        "offs": striped(np.random.permutation(T)[:S]),
        "two": striped(np.random.permutation(T)[:S]),
        "n1": striped(np.random.permutation(S)),
        "n2": striped(np.random.permutation(S)),
        "three": striped(np.random.permutation(T)[:V]),
        "n3": striped8(np.stack([np.random.permutation(V) for _ in range(8)])),
        "n4": striped8(np.stack([np.random.permutation(V) for _ in range(8)])),
        "n5": striped8(np.stack([np.random.permutation(V) for _ in range(8)])),
        "n6": striped8(np.random.randint(0, J, (8, V))),
        "n7": striped8(np.random.randint(0, J, (8, V))),
        "n8": striped8(np.stack([np.random.permutation(V) for _ in range(8)])),
    }


def reference(x_words, x_scales, w1_words, w1_scales, w2_words, w2_scales, w3_words, w3_scales, ga, gb, tab, offs, two, n1, n2, three, n3, n4, n5, n6, n7, n8):
    xq = unpack_weight(x_words, x_scales)[:, unstriped(offs)]
    y = unpack_fp4(w1_words, w1_scales).T @ xq
    x_two = unpack_weight(x_words, x_scales)[:, unstriped(two)]
    d = unpack_fp4(w2_words, w2_scales).T @ x_two
    z = f64(ga) * ((y - y[:, unstriped(n1)]) / (np.abs(d) + np.abs(d[:, unstriped(n2)]) + 0.5))
    x_three = unpack_weight(x_words, x_scales)[:, unstriped(three)]
    b = unpack_fp4(w3_words, w3_scales).T @ x_three
    z2 = f64(gb) * ((b[np.arange(H)[:, None], runs(n3, H)]) * sigmoid(b) + (b[np.arange(H)[:, None], runs(n4, H)]) * (sigmoid(b[np.arange(H)[:, None], runs(n5, H)])))
    s = 0.0625 * ((mxq(z, 0, "e4m3").T @ mxq(z2, 0, "e4m3")))
    out_0 = (s[np.arange(S)[:, None], runs(n8, S)]) * (f64(tab)[np.arange(S)[:, None], runs(n6, S)]) + f64(tab)[np.arange(S)[:, None], runs(n7, S)]
    return (out_0,) + planes(out_0)

@@ -1,0 +1,268 @@
+from contextlib import ExitStack
+
+import concourse.mybir as mybir
+from concourse.masks import make_identity
+
+K, T, S, V, H, J = 512, 2048, 512, 256, 512, 512
+P = 128
+PACK = 4
+FLOPS = 2 * K * H * (S + S + V) + 2 * H * S * V
+
+F32 = mybir.dt.float32
+BF16 = mybir.dt.bfloat16
+I32 = mybir.dt.int32
+U32 = mybir.dt.uint32
+U16 = mybir.dt.uint16
+U8 = mybir.dt.uint8
+FP8X4 = mybir.dt.float8_e4m3fn_x4
+FP4X4 = mybir.dt.float4_e2m1fn_x4
+ALU = mybir.AluOpType
+ACT = mybir.ActivationFunctionType
+
+Y_WINDOW = S + 16
+D_WINDOW = S + 192
+Q_WINDOW = 2 * V
+LN_FLOOR = 2.0 ** -60
+
+
+def tile_picked_twknormbwsumkinda_none_po_kernel(
+    tc, x_words, x_scales, w1_words, w1_scales, w2_words, w2_scales, w3_words, w3_scales,
+    ga, gb, tab, offs, two, n1, n2, three, n3, n4, n5, n6, n7, n8, out_0, out_1, out_2,
+):
+    nc = tc.nc
+    with ExitStack() as ctx:
+        keep = ctx.enter_context(tc.tile_pool(name="keep", bufs=1))
+        acc = ctx.enter_context(tc.psum_pool(name="acc", bufs=2))
+        turned = ctx.enter_context(tc.psum_pool(name="turned", bufs=6))
+
+        def sbuf(name, shape, dtype, tag=""):
+            return keep.tile(shape, dtype, name=name, tag=tag or name, align_bytes=64)
+
+        lists = {}
+
+        def load_list(name, dram):
+            lists[name] = sbuf("list_" + name, list(dram.shape), U16)
+            nc.sync.dma_start(lists[name][:], dram)
+
+        def load_scales(tile, dram):
+            for q in range(4):
+                nc.sync.dma_start(tile[32 * q : 32 * q + 4, :].bitcast(I32), dram[0, 4 * q : 4 * q + 4, :].bitcast(I32))
+
+        def load_fp4(name, dram):
+            tile = sbuf(name, [P, 2 * H], U8)
+            nc.sync.dma_start(tile[:].bitcast(I32), dram[0].bitcast(I32))
+            return tile
+
+        xs = sbuf("xs", [P, T], U8)
+        w1s = sbuf("w1s", [P, H], U8)
+        w2s = sbuf("w2s", [P, H], U8)
+        w3s_raw = sbuf("w3s_raw", [P, H], U8)
+        nc.vector.memset(xs[:].bitcast(I32), 0)
+        for tile in (w2s, w1s, w3s_raw):
+            nc.vector.memset(tile[:].bitcast(I32), 0)
+
+        tab_rows = tab.rearrange("(p t) j -> t p j", t=PACK)
+        tabs = [sbuf("tab%d" % t, [P, J], F32) for t in range(PACK)]
+        xw = sbuf("xw", [P, T], U32)
+        ga_sb = sbuf("ga_sb", [P, PACK], F32)
+        gb_sb = sbuf("gb_sb", [P, PACK], F32)
+
+        load_list("two", two)
+        nc.sync.dma_start(xw[:].bitcast(I32), x_words[0].rearrange("p n t -> p (n t)").bitcast(I32))
+        load_scales(xs, x_scales)
+        w2w = load_fp4("w2w", w2_words)
+        nc.sync.dma_start(tabs[0][:], tab_rows[0])
+        load_scales(w2s, w2_scales)
+        load_list("n6", n6)
+        load_list("n7", n7)
+        load_list("offs", offs)
+        nc.sync.dma_start(tabs[1][:], tab_rows[1])
+        w1w = load_fp4("w1w", w1_words)
+        load_scales(w1s, w1_scales)
+        with nc.allow_non_contiguous_dma(reason="one weight a partition and feature tile"):
+            nc.sync.dma_start(ga_sb[:], ga.rearrange("(f p) o -> p (f o)", p=P))
+        load_list("n2", n2)
+        load_list("n1", n1)
+        w3w_raw = load_fp4("w3w_raw", w3_words)
+        load_scales(w3s_raw, w3_scales)
+        load_list("three", three)
+        nc.sync.dma_start(tabs[2][:], tab_rows[2])
+        nc.sync.dma_start(tabs[3][:], tab_rows[3])
+        nc.sync.dma_start(gb_sb[:], gb.rearrange("(p t) o -> p (t o)", t=PACK))
+        for name, dram in (("n3", n3), ("n4", n4), ("n5", n5), ("n8", n8)):
+            load_list(name, dram)
+
+        ident = sbuf("ident", [P, P], F32)
+        make_identity(nc, ident[:])
+        ln_floor = sbuf("ln_floor", [P, 1], F32, tag="after_ln")
+        nc.gpsimd.memset(ln_floor[:], LN_FLOOR)
+
+        def window(name, used, width):
+            tile = sbuf(name, [P, width], F32)
+            nc.gpsimd.memset(tile[:, used:], 0.0)
+            return tile
+
+        d_abs = [window("d_abs%d" % f, S, D_WINDOW) for f in range(4)]
+        y_win = [window("y_win%d" % f, S, Y_WINDOW) for f in range(4)]
+        b_win = [window("b_win%d" % t, V, Q_WINDOW) for t in range(PACK)]
+        s_win = [window("s_win%d" % t, V, Q_WINDOW) for t in range(PACK)]
+
+        w3w = sbuf("w3w", [P, 2 * H], U8)
+        w3s = sbuf("w3s", [P, H], U8)
+        nc.gpsimd.tensor_copy(
+            w3w[:].rearrange("p (t m b) -> p t m b", t=PACK, b=2),
+            w3w_raw[:].rearrange("p (m t b) -> p t m b", t=PACK, b=2),
+        )
+        nc.gpsimd.tensor_copy(
+            w3s[:].rearrange("p (t m) -> p t m", t=PACK),
+            w3s_raw[:].rearrange("p (m t) -> p t m", t=PACK),
+        )
+
+        def pick(name, width):
+            words = sbuf("words_" + name, [P, width], U32)
+            scales = sbuf("scales_" + name, [P, width], U8)
+            nc.vector.tensor_copy(words[:], xw[:].indirect(lists[name][:]))
+            nc.vector.tensor_copy(scales[:], xs[:].indirect(lists[name][:]))
+            return words, scales
+
+        def project(out, w_words, w_scales, tile, picked):
+            nc.tensor.matmul_mx(
+                out,
+                lhsT=w_words[:, 2 * P * tile : 2 * P * (tile + 1)].bitcast(FP4X4),
+                lhsT_scale=w_scales[:, P * tile : P * (tile + 1)],
+                rhs=picked[0][:].bitcast(FP8X4),
+                rhs_scale=picked[1][:],
+                start=True,
+                stop=True,
+            )
+
+        def turn_and_add(name, first, second):
+            bank = turned.tile([P, 4, P], F32, name=name, tag="turned")
+            for u in range(4):
+                cols = slice(P * u, P * (u + 1))
+                nc.tensor.matmul(bank[:, u, :], lhsT=first[:, cols], rhs=ident[:], is_transpose=True, start=True, stop=False)
+                nc.tensor.matmul(bank[:, u, :], lhsT=second[:, cols], rhs=ident[:], is_transpose=True, start=False, stop=True)
+            return bank
+
+        x_two = pick("two", S)
+        x_offs = pick("offs", S)
+
+        for f in range(4):
+            bank = acc.tile([P, S], F32, name="d_acc%d" % f, tag="acc")
+            project(bank[:], w2w, w2s, f, x_two)
+            nc.scalar.activation(d_abs[f][:, :S], bank[:], ACT.Abs)
+        for f in range(4):
+            bank = acc.tile([P, S], F32, name="y_acc%d" % f, tag="acc")
+            project(bank[:], w1w, w1s, f, x_offs)
+            nc.vector.tensor_scalar(y_win[f][:, :S], bank[:], ga_sb[:, f : f + 1], 2.0, ALU.mult, ALU.mult)
+
+        ln_sum = sbuf("ln_sum", [P, 4, S], F32)
+        for f in range(4):
+            d_n2 = sbuf("d_n2_%d" % f, [P, S], F32)
+            nc.vector.tensor_copy(d_n2[:], d_abs[f][:].indirect(lists["n2"][:]))
+            bank = turn_and_add("sum_t%d" % f, d_abs[f], d_n2)
+            nc.scalar.activation(ln_sum[:, f, :], bank[:].rearrange("p u c -> p (u c)"), ACT.Ln, bias=ln_floor[:], scale=2.0)
+        diff = []
+        for f in range(4):
+            y_n1 = sbuf("y_n1_%d" % f, [P, S], F32)
+            nc.scalar.activation(y_n1[:], y_win[f][:].indirect(lists["n1"][:]), ACT.Copy, scale=-1.0)
+            diff.append(turn_and_add("diff_t%d" % f, y_win[f], y_n1))
+
+        x_three = pick("three", V)
+        for pair in range(2):
+            bank = acc.tile([P, 2, V], F32, name="b_acc%d" % pair, tag="acc")
+            for i in range(2):
+                project(bank[:, i, :], w3w, w3s, 2 * pair + i, x_three)
+            for i in range(2):
+                nc.vector.tensor_copy(b_win[2 * pair + i][:, :V], bank[:, i, :])
+
+        sig = sbuf("sig", [P, 4 * S + 2 * PACK * V], F32, tag="after_ln")
+        z_t = sbuf("z_t", [P, 4, H], BF16)
+        for f in range(4):
+            rec = sig[:, S * f : S * (f + 1)]
+            nc.scalar.activation(rec, ln_sum[:, f, :], ACT.Sigmoid, scale=-1.0)
+            nc.vector.tensor_tensor(z_t[:, :, P * f : P * (f + 1)], diff[f][:], rec.rearrange("p (u c) -> p u c", u=4), ALU.mult)
+
+        z_grouped = sbuf("z_grouped", [P, PACK * S], BF16)
+        z_grouped_words = z_grouped[:].bitcast(F32).rearrange("p (t u m h) -> p u t m h", t=PACK, u=4, h=2)
+        for pair in range(2):
+            bank = acc.tile([P, 2, 2, P], F32, name="z_back%d" % pair, tag="acc")
+            for i in range(2):
+                words = z_t[:, 2 * pair + i, :].bitcast(F32)
+                for h in range(2):
+                    nc.tensor.transpose(bank[:, i, h, :], words[:, h::2], ident[:])
+            nc.vector.tensor_copy(
+                z_grouped_words[:, 2 * pair : 2 * pair + 2],
+                bank[:].rearrange("p i h (m t) -> p i t m h", t=PACK),
+            )
+        z_words = sbuf("z_words", [P, S], U32)
+        z_scales = sbuf("z_scales", [P, S], U8)
+        nc.vector.quantize_mx(z_words[:].bitcast(FP8X4), z_scales[:], z_grouped[:])
+
+        z2 = sbuf("z2", [P, PACK, V], F32)
+        for t in range(PACK):
+            sig_b = sig[:, 4 * S + V * t : 4 * S + V * (t + 1)]
+            sig_n5 = sig[:, 4 * S + PACK * V + V * t : 4 * S + PACK * V + V * (t + 1)]
+            b_n3 = sbuf("b_n3_%d" % t, [P, V], F32)
+            b_n4 = sbuf("b_n4_%d" % t, [P, V], F32)
+            left = sbuf("left%d" % t, [P, V], F32)
+            right = sbuf("right%d" % t, [P, V], F32)
+            nc.scalar.activation(b_n3[:], b_win[t][:].indirect(lists["n3"][:]), ACT.Copy)
+            nc.scalar.activation(sig_b, b_win[t][:, :V], ACT.Sigmoid)
+            nc.scalar.activation(b_n4[:], b_win[t][:].indirect(lists["n4"][:]), ACT.Copy)
+            nc.scalar.activation(sig_n5, b_win[t][:].indirect(lists["n5"][:]), ACT.Sigmoid)
+            nc.vector.scalar_tensor_tensor(left[:], b_n3[:], gb_sb[:, t : t + 1], sig_b, ALU.mult, ALU.mult)
+            nc.vector.scalar_tensor_tensor(right[:], b_n4[:], gb_sb[:, t : t + 1], sig_n5, ALU.mult, ALU.mult)
+            nc.vector.tensor_tensor(z2[:, t, :], left[:], right[:], ALU.add)
+        z2_grouped = sbuf("z2_grouped", [P, V, PACK], BF16)
+        nc.vector.tensor_copy(
+            z2_grouped[:].rearrange("p (c i) t -> p c t i", i=4), z2[:].rearrange("p t (c i) -> p c t i", i=4)
+        )
+        z2_words = sbuf("z2_words", [P, V], U32)
+        z2_scales = sbuf("z2_scales", [P, V], U8)
+        nc.vector.quantize_mx(z2_words[:].bitcast(FP8X4), z2_scales[:], z2_grouped[:].rearrange("p c t -> p (c t)"))
+
+        tab_n6 = [sbuf("tab_n6_%d" % t, [P, V], F32) for t in range(PACK)]
+        tab_n7 = [sbuf("tab_n7_%d" % t, [P, V], F32) for t in range(PACK)]
+        for t in range(PACK):
+            for name, tile in (("n6", tab_n6[t]), ("n7", tab_n7[t])):
+                if t < 2:
+                    nc.scalar.activation(tile[:], tabs[t][:].indirect(lists[name][:]), ACT.Copy)
+                else:
+                    nc.vector.tensor_copy(tile[:], tabs[t][:].indirect(lists[name][:]))
+
+        result = sbuf("result", [P, PACK, V], F32)
+        out_rows = out_0.rearrange("(p t) v -> p t v", t=PACK)
+        for pair in range(2):
+            bank = acc.tile([P, 2, V], F32, name="s_acc%d" % pair, tag="acc")
+            for i in range(2):
+                cols = slice(P * (2 * pair + i), P * (2 * pair + i + 1))
+                nc.tensor.matmul_mx(
+                    bank[:, i, :],
+                    lhsT=z_words[:, cols].bitcast(FP8X4),
+                    lhsT_scale=z_scales[:, cols],
+                    rhs=z2_words[:].bitcast(FP8X4),
+                    rhs_scale=z2_scales[:],
+                    start=True,
+                    stop=True,
+                )
+            for i in range(2):
+                nc.vector.tensor_scalar(s_win[2 * pair + i][:, :V], bank[:, i, :], 0.0625, None, ALU.mult)
+        for t in range(PACK):
+            s_n8 = sbuf("s_n8_%d" % t, [P, V], F32)
+            scaled = sbuf("scaled%d" % t, [P, V], F32)
+            nc.scalar.activation(s_n8[:], s_win[t][:].indirect(lists["n8"][:]), ACT.Copy)
+            nc.vector.tensor_tensor(scaled[:], s_n8[:], tab_n6[t][:], ALU.mult)
+            nc.vector.tensor_tensor(result[:, t, :], scaled[:], tab_n7[t][:], ALU.add)
+            nc.sync.dma_start(out_rows[:, t, :], result[:, t, :])
+
+        out_grouped = sbuf("out_grouped", [P, V, PACK], BF16)
+        nc.vector.tensor_copy(
+            out_grouped[:].rearrange("p (c i) t -> p c t i", i=4), result[:].rearrange("p t (c i) -> p c t i", i=4)
+        )
+        out_words = sbuf("out_words", [P, V], U32)
+        out_scales = sbuf("out_scales", [P, V], U8)
+        nc.vector.quantize_mx(out_words[:].bitcast(FP8X4), out_scales[:], out_grouped[:].rearrange("p c t -> p (c t)"))
+        nc.sync.dma_start(out_1[0].rearrange("p n t -> p (n t)").bitcast(I32), out_words[:].bitcast(I32))
+        for q in range(4):
+            nc.sync.dma_start(out_2[0, 4 * q : 4 * q + 4, :].bitcast(I32), out_scales[32 * q : 32 * q + 4, :].bitcast(I32))

@@ -20,7 +20,6 @@ ALU = mybir.AluOpType
 ACT = mybir.ActivationFunctionType
 
 Y_WINDOW = S + 16
-D_WINDOW = S + 192
 Q_WINDOW = 2 * V
 LN_FLOOR = 2.0 ** -60
 
@@ -32,11 +31,13 @@ def tile_picked_twknormbwsumkinda_none_po_kernel(
     nc = tc.nc
     with ExitStack() as ctx:
         keep = ctx.enter_context(tc.tile_pool(name="keep", bufs=1))
-        acc = ctx.enter_context(tc.psum_pool(name="acc", bufs=2))
-        turned = ctx.enter_context(tc.psum_pool(name="turned", bufs=6))
+        psum = ctx.enter_context(tc.psum_pool(name="psum", bufs=1))
 
         def sbuf(name, shape, dtype, tag=""):
             return keep.tile(shape, dtype, name=name, tag=tag or name, align_bytes=64)
+
+        def bank(name, number, shape):
+            return psum.tile(shape, F32, name=name, tag="bank%d" % number)
 
         lists = {}
 
@@ -44,9 +45,9 @@ def tile_picked_twknormbwsumkinda_none_po_kernel(
             lists[name] = sbuf("list_" + name, list(dram.shape), U16)
             nc.sync.dma_start(lists[name][:], dram)
 
-        def load_scales(tile, dram):
+        def load_scales(queue, tile, dram):
             for q in range(4):
-                nc.sync.dma_start(tile[32 * q : 32 * q + 4, :].bitcast(I32), dram[0, 4 * q : 4 * q + 4, :].bitcast(I32))
+                queue.dma_start(tile[32 * q : 32 * q + 4, :].bitcast(I32), dram[0, 4 * q : 4 * q + 4, :].bitcast(I32))
 
         def load_fp4(name, dram):
             tile = sbuf(name, [P, 2 * H], U8)
@@ -57,9 +58,12 @@ def tile_picked_twknormbwsumkinda_none_po_kernel(
         w1s = sbuf("w1s", [P, H], U8)
         w2s = sbuf("w2s", [P, H], U8)
         w3s_raw = sbuf("w3s_raw", [P, H], U8)
-        nc.vector.memset(xs[:].bitcast(I32), 0)
-        for tile in (w2s, w1s, w3s_raw):
-            nc.vector.memset(tile[:].bitcast(I32), 0)
+        half = sbuf("half", [P, 1], F32)
+        nc.gpsimd.memset(xs[:].bitcast(I32), 0)
+        nc.gpsimd.memset(w2s[:].bitcast(I32), 0)
+        nc.vector.memset(half[:], 0.5)
+        nc.vector.memset(w1s[:].bitcast(I32), 0)
+        nc.vector.memset(w3s_raw[:].bitcast(I32), 0)
 
         tab_rows = tab.rearrange("(p t) j -> t p j", t=PACK)
         tabs = [sbuf("tab%d" % t, [P, J], F32) for t in range(PACK)]
@@ -67,62 +71,55 @@ def tile_picked_twknormbwsumkinda_none_po_kernel(
         ga_sb = sbuf("ga_sb", [P, PACK], F32)
         gb_sb = sbuf("gb_sb", [P, PACK], F32)
 
+        nc.scalar.dma_start(xw[:].bitcast(I32), x_words[0].rearrange("p n t -> p (n t)").bitcast(I32))
         load_list("two", two)
-        nc.sync.dma_start(xw[:].bitcast(I32), x_words[0].rearrange("p n t -> p (n t)").bitcast(I32))
-        load_scales(xs, x_scales)
-        w2w = load_fp4("w2w", w2_words)
-        nc.sync.dma_start(tabs[0][:], tab_rows[0])
-        load_scales(w2s, w2_scales)
-        load_list("n6", n6)
-        load_list("n7", n7)
+        load_scales(nc.sync, xs, x_scales)
+        load_scales(nc.gpsimd, w2s, w2_scales)
         load_list("offs", offs)
-        nc.sync.dma_start(tabs[1][:], tab_rows[1])
+        w2w = load_fp4("w2w", w2_words)
         w1w = load_fp4("w1w", w1_words)
-        load_scales(w1s, w1_scales)
+        load_scales(nc.sync, w1s, w1_scales)
         with nc.allow_non_contiguous_dma(reason="one weight a partition and feature tile"):
             nc.sync.dma_start(ga_sb[:], ga.rearrange("(f p) o -> p (f o)", p=P))
+        nc.sync.dma_start(tabs[0][:], tab_rows[0])
+        load_list("n6", n6)
+        load_list("n7", n7)
+        w3w_raw = load_fp4("w3w_raw", w3_words)
+        load_scales(nc.sync, w3s_raw, w3_scales)
         load_list("n2", n2)
         load_list("n1", n1)
-        w3w_raw = load_fp4("w3w_raw", w3_words)
-        load_scales(w3s_raw, w3_scales)
         load_list("three", three)
-        nc.sync.dma_start(tabs[2][:], tab_rows[2])
-        nc.sync.dma_start(tabs[3][:], tab_rows[3])
         nc.sync.dma_start(gb_sb[:], gb.rearrange("(p t) o -> p (t o)", t=PACK))
         for name, dram in (("n3", n3), ("n4", n4), ("n5", n5), ("n8", n8)):
             load_list(name, dram)
+        for t in range(1, PACK):
+            nc.sync.dma_start(tabs[t][:], tab_rows[t])
 
+        ln_half = sbuf("ln_half", [P, 1], F32)
+        nc.scalar.activation(ln_half[:], half[:], ACT.Ln)
         ident = sbuf("ident", [P, P], F32)
         make_identity(nc, ident[:])
         ln_floor = sbuf("ln_floor", [P, 1], F32, tag="after_ln")
-        nc.gpsimd.memset(ln_floor[:], LN_FLOOR)
+        nc.vector.memset(ln_floor[:], LN_FLOOR)
 
         def window(name, used, width):
             tile = sbuf(name, [P, width], F32)
-            nc.gpsimd.memset(tile[:, used:], 0.0)
+            nc.vector.memset(tile[:, used:], 0.0)
             return tile
 
-        d_abs = [window("d_abs%d" % f, S, D_WINDOW) for f in range(4)]
+        d_abs = [sbuf("d_abs%d" % f, [P, S], F32) for f in range(4)]
         y_win = [window("y_win%d" % f, S, Y_WINDOW) for f in range(4)]
         b_win = [window("b_win%d" % t, V, Q_WINDOW) for t in range(PACK)]
-        s_win = [window("s_win%d" % t, V, Q_WINDOW) for t in range(PACK)]
+        s_win = b_win
 
         w3w = sbuf("w3w", [P, 2 * H], U8)
         w3s = sbuf("w3s", [P, H], U8)
-        nc.gpsimd.tensor_copy(
-            w3w[:].rearrange("p (t m b) -> p t m b", t=PACK, b=2),
-            w3w_raw[:].rearrange("p (m t b) -> p t m b", t=PACK, b=2),
-        )
-        nc.gpsimd.tensor_copy(
-            w3s[:].rearrange("p (t m) -> p t m", t=PACK),
-            w3s_raw[:].rearrange("p (m t) -> p t m", t=PACK),
-        )
 
         def pick(name, width):
             words = sbuf("words_" + name, [P, width], U32)
             scales = sbuf("scales_" + name, [P, width], U8)
-            nc.vector.tensor_copy(words[:], xw[:].indirect(lists[name][:]))
             nc.vector.tensor_copy(scales[:], xs[:].indirect(lists[name][:]))
+            nc.vector.tensor_copy(words[:], xw[:].indirect(lists[name][:]))
             return words, scales
 
         def project(out, w_words, w_scales, tile, picked):
@@ -136,84 +133,142 @@ def tile_picked_twknormbwsumkinda_none_po_kernel(
                 stop=True,
             )
 
-        def turn_and_add(name, first, second):
-            bank = turned.tile([P, 4, P], F32, name=name, tag="turned")
+        def turn_and_add(name, number, first, second):
+            acc = bank(name, number, [P, 4, P])
             for u in range(4):
                 cols = slice(P * u, P * (u + 1))
-                nc.tensor.matmul(bank[:, u, :], lhsT=first[:, cols], rhs=ident[:], is_transpose=True, start=True, stop=False)
-                nc.tensor.matmul(bank[:, u, :], lhsT=second[:, cols], rhs=ident[:], is_transpose=True, start=False, stop=True)
-            return bank
+                nc.tensor.matmul(acc[:, u, :], lhsT=first[:, cols], rhs=ident[:], is_transpose=True, start=True, stop=False)
+                nc.tensor.matmul(acc[:, u, :], lhsT=second[:, cols], rhs=ident[:], is_transpose=True, start=False, stop=True)
+            return acc
+
+        def tab_gather(engine, name, t, out):
+            looked_up = tabs[t][:].indirect(lists[name][:])
+            if engine is nc.scalar:
+                nc.scalar.activation(out, looked_up, ACT.Copy)
+            else:
+                nc.vector.tensor_copy(out, looked_up)
 
         x_two = pick("two", S)
+        for f in range(4):
+            acc = bank("d_acc%d" % f, f, [P, S])
+            project(acc[:], w2w, w2s, f, x_two)
+            nc.scalar.activation(d_abs[f][:], acc[:], ACT.Abs)
         x_offs = pick("offs", S)
+        y_acc = []
+        for f in range(4):
+            y_acc.append(bank("y_acc%d" % f, 4 + f, [P, S]))
+            project(y_acc[f][:], w1w, w1s, f, x_offs)
 
-        for f in range(4):
-            bank = acc.tile([P, S], F32, name="d_acc%d" % f, tag="acc")
-            project(bank[:], w2w, w2s, f, x_two)
-            nc.scalar.activation(d_abs[f][:, :S], bank[:], ACT.Abs)
-        for f in range(4):
-            bank = acc.tile([P, S], F32, name="y_acc%d" % f, tag="acc")
-            project(bank[:], w1w, w1s, f, x_offs)
-            nc.vector.tensor_scalar(y_win[f][:, :S], bank[:], ga_sb[:, f : f + 1], 2.0, ALU.mult, ALU.mult)
+        tab_at = {}
+        for name in ("n6", "n7"):
+            tab_at[name, 0] = sbuf("tab_%s_0" % name, [P, V], F32)[:]
+            tab_gather(nc.scalar, name, 0, tab_at[name, 0])
 
         ln_sum = sbuf("ln_sum", [P, 4, S], F32)
-        for f in range(4):
+        sums = {}
+        diff = {}
+
+        def denominator(f):
             d_n2 = sbuf("d_n2_%d" % f, [P, S], F32)
-            nc.vector.tensor_copy(d_n2[:], d_abs[f][:].indirect(lists["n2"][:]))
-            bank = turn_and_add("sum_t%d" % f, d_abs[f], d_n2)
-            nc.scalar.activation(ln_sum[:, f, :], bank[:].rearrange("p u c -> p (u c)"), ACT.Ln, bias=ln_floor[:], scale=2.0)
-        diff = []
-        for f in range(4):
+            for i in range(2):
+                nc.vector.tensor_copy(d_n2[:, 256 * i : 256 * (i + 1)], d_abs[f][:].indirect(lists["n2"][:, 16 * i : 16 * (i + 1)]))
+            sums[f] = turn_and_add("sum_t%d" % f, f, d_abs[f], d_n2)
+
+        def logarithm(f):
+            nc.scalar.activation(ln_sum[:, f, :], sums[f][:].rearrange("p u c -> p (u c)"), ACT.Ln, bias=ln_floor[:])
+
+        def y_out(f):
+            nc.vector.tensor_scalar(y_win[f][:, :S], y_acc[f][:], ga_sb[:, f : f + 1], 2.0, ALU.mult, ALU.mult)
+
+        def numerator(f):
             y_n1 = sbuf("y_n1_%d" % f, [P, S], F32)
             nc.scalar.activation(y_n1[:], y_win[f][:].indirect(lists["n1"][:]), ACT.Copy, scale=-1.0)
-            diff.append(turn_and_add("diff_t%d" % f, y_win[f], y_n1))
+            diff[f] = turn_and_add("diff_t%d" % f, 4 + f, y_win[f], y_n1)
 
+        denominator(0)
+        y_out(0)
+        y_out(1)
+        numerator(0)
+        logarithm(0)
+        denominator(1)
+        y_out(2)
+        y_out(3)
+        numerator(1)
+        logarithm(1)
+        denominator(2)
+        numerator(2)
+        denominator(3)
+        logarithm(2)
+        numerator(3)
+        logarithm(3)
+
+        nc.vector.tensor_copy(
+            w3w[:].rearrange("p (t m b) -> p t m b", t=PACK, b=2),
+            w3w_raw[:].rearrange("p (m t b) -> p t m b", t=PACK, b=2),
+        )
+        nc.vector.tensor_copy(
+            w3s[:].rearrange("p (t m) -> p t m", t=PACK),
+            w3s_raw[:].rearrange("p (m t) -> p t m", t=PACK),
+        )
         x_three = pick("three", V)
+        for t in range(2, PACK):
+            for name in ("n6", "n7"):
+                tab_at[name, t] = sbuf("tab_%s_%d" % (name, t), [P, V], F32)[:]
+        b_acc = []
         for pair in range(2):
-            bank = acc.tile([P, 2, V], F32, name="b_acc%d" % pair, tag="acc")
+            b_acc.append(bank("b_acc%d" % pair, pair, [P, 2, V]))
             for i in range(2):
-                project(bank[:, i, :], w3w, w3s, 2 * pair + i, x_three)
-            for i in range(2):
-                nc.vector.tensor_copy(b_win[2 * pair + i][:, :V], bank[:, i, :])
+                project(b_acc[pair][:, i, :], w3w, w3s, 2 * pair + i, x_three)
+        for t in range(PACK):
+            nc.vector.tensor_copy(b_win[t][:, :V], b_acc[t // 2][:, t % 2, :])
+        for t in range(2, PACK):
+            for name in ("n6", "n7"):
+                tab_gather(nc.vector, name, t, tab_at[name, t])
 
-        sig = sbuf("sig", [P, 4 * S + 2 * PACK * V], F32, tag="after_ln")
+        late = sbuf("late", [P, 4 * S + (4 * PACK + 2) * V], F32, tag="after_ln")
+
+        def late_cols(i):
+            return late[:, 4 * S + V * i : 4 * S + V * (i + 1)]
+
         z_t = sbuf("z_t", [P, 4, H], BF16)
         for f in range(4):
-            rec = sig[:, S * f : S * (f + 1)]
-            nc.scalar.activation(rec, ln_sum[:, f, :], ACT.Sigmoid, scale=-1.0)
+            rec = late[:, S * f : S * (f + 1)]
+            nc.scalar.activation(rec, ln_sum[:, f, :], ACT.Sigmoid, bias=ln_half[:], scale=-1.0)
             nc.vector.tensor_tensor(z_t[:, :, P * f : P * (f + 1)], diff[f][:], rec.rearrange("p (u c) -> p u c", u=4), ALU.mult)
 
         z_grouped = sbuf("z_grouped", [P, PACK * S], BF16)
         z_grouped_words = z_grouped[:].bitcast(F32).rearrange("p (t u m h) -> p u t m h", t=PACK, u=4, h=2)
+        z_back = []
         for pair in range(2):
-            bank = acc.tile([P, 2, 2, P], F32, name="z_back%d" % pair, tag="acc")
+            z_back.append(bank("z_back%d" % pair, 2 + pair, [P, 2, 2, P]))
             for i in range(2):
                 words = z_t[:, 2 * pair + i, :].bitcast(F32)
                 for h in range(2):
-                    nc.tensor.transpose(bank[:, i, h, :], words[:, h::2], ident[:])
-            nc.vector.tensor_copy(
-                z_grouped_words[:, 2 * pair : 2 * pair + 2],
-                bank[:].rearrange("p i h (m t) -> p i t m h", t=PACK),
-            )
+                    nc.tensor.transpose(z_back[pair][:, i, h, :], words[:, h::2], ident[:])
+
         z_words = sbuf("z_words", [P, S], U32)
         z_scales = sbuf("z_scales", [P, S], U8)
-        nc.vector.quantize_mx(z_words[:].bitcast(FP8X4), z_scales[:], z_grouped[:])
-
         z2 = sbuf("z2", [P, PACK, V], F32)
         for t in range(PACK):
-            sig_b = sig[:, 4 * S + V * t : 4 * S + V * (t + 1)]
-            sig_n5 = sig[:, 4 * S + PACK * V + V * t : 4 * S + PACK * V + V * (t + 1)]
-            b_n3 = sbuf("b_n3_%d" % t, [P, V], F32)
-            b_n4 = sbuf("b_n4_%d" % t, [P, V], F32)
+            b_n3, sig_b, b_n4, sig_n5 = [late_cols(4 * t + i) for i in range(4)]
             left = sbuf("left%d" % t, [P, V], F32)
             right = sbuf("right%d" % t, [P, V], F32)
-            nc.scalar.activation(b_n3[:], b_win[t][:].indirect(lists["n3"][:]), ACT.Copy)
+            nc.scalar.activation(b_n3, b_win[t][:].indirect(lists["n3"][:]), ACT.Copy)
             nc.scalar.activation(sig_b, b_win[t][:, :V], ACT.Sigmoid)
-            nc.scalar.activation(b_n4[:], b_win[t][:].indirect(lists["n4"][:]), ACT.Copy)
+            nc.scalar.activation(b_n4, b_win[t][:].indirect(lists["n4"][:]), ACT.Copy)
             nc.scalar.activation(sig_n5, b_win[t][:].indirect(lists["n5"][:]), ACT.Sigmoid)
-            nc.vector.scalar_tensor_tensor(left[:], b_n3[:], gb_sb[:, t : t + 1], sig_b, ALU.mult, ALU.mult)
-            nc.vector.scalar_tensor_tensor(right[:], b_n4[:], gb_sb[:, t : t + 1], sig_n5, ALU.mult, ALU.mult)
+            nc.vector.scalar_tensor_tensor(left[:], b_n3, gb_sb[:, t : t + 1], sig_b, ALU.mult, ALU.mult)
+            if t < 2:
+                nc.vector.tensor_copy(
+                    z_grouped_words[:, 2 * t : 2 * t + 2], z_back[t][:].rearrange("p i h (m t) -> p i t m h", t=PACK)
+                )
+            if t == 2:
+                nc.vector.quantize_mx(z_words[:].bitcast(FP8X4), z_scales[:], z_grouped[:])
+            nc.vector.scalar_tensor_tensor(right[:], b_n4, gb_sb[:, t : t + 1], sig_n5, ALU.mult, ALU.mult)
             nc.vector.tensor_tensor(z2[:, t, :], left[:], right[:], ALU.add)
+        for i, name in enumerate(("n6", "n7")):
+            tab_at[name, 1] = late_cols(4 * PACK + i)
+            tab_gather(nc.scalar, name, 1, tab_at[name, 1])
         z2_grouped = sbuf("z2_grouped", [P, V, PACK], BF16)
         nc.vector.tensor_copy(
             z2_grouped[:].rearrange("p (c i) t -> p c t i", i=4), z2[:].rearrange("p t (c i) -> p c t i", i=4)
@@ -222,38 +277,30 @@ def tile_picked_twknormbwsumkinda_none_po_kernel(
         z2_scales = sbuf("z2_scales", [P, V], U8)
         nc.vector.quantize_mx(z2_words[:].bitcast(FP8X4), z2_scales[:], z2_grouped[:].rearrange("p c t -> p (c t)"))
 
-        tab_n6 = [sbuf("tab_n6_%d" % t, [P, V], F32) for t in range(PACK)]
-        tab_n7 = [sbuf("tab_n7_%d" % t, [P, V], F32) for t in range(PACK)]
-        for t in range(PACK):
-            for name, tile in (("n6", tab_n6[t]), ("n7", tab_n7[t])):
-                if t < 2:
-                    nc.scalar.activation(tile[:], tabs[t][:].indirect(lists[name][:]), ACT.Copy)
-                else:
-                    nc.vector.tensor_copy(tile[:], tabs[t][:].indirect(lists[name][:]))
-
         result = sbuf("result", [P, PACK, V], F32)
         out_rows = out_0.rearrange("(p t) v -> p t v", t=PACK)
-        for pair in range(2):
-            bank = acc.tile([P, 2, V], F32, name="s_acc%d" % pair, tag="acc")
-            for i in range(2):
-                cols = slice(P * (2 * pair + i), P * (2 * pair + i + 1))
-                nc.tensor.matmul_mx(
-                    bank[:, i, :],
-                    lhsT=z_words[:, cols].bitcast(FP8X4),
-                    lhsT_scale=z_scales[:, cols],
-                    rhs=z2_words[:].bitcast(FP8X4),
-                    rhs_scale=z2_scales[:],
-                    start=True,
-                    stop=True,
-                )
-            for i in range(2):
-                nc.vector.tensor_scalar(s_win[2 * pair + i][:, :V], bank[:, i, :], 0.0625, None, ALU.mult)
+        for t in range(PACK):
+            acc = bank("s_acc%d" % t, 4 + t, [P, V])
+            cols = slice(P * t, P * (t + 1))
+            nc.tensor.matmul_mx(
+                acc[:],
+                lhsT=z_words[:, cols].bitcast(FP8X4),
+                lhsT_scale=z_scales[:, cols],
+                rhs=z2_words[:].bitcast(FP8X4),
+                rhs_scale=z2_scales[:],
+                start=True,
+                stop=True,
+            )
+            if t == 0:
+                nc.scalar.activation(s_win[t][:, :V], acc[:], ACT.Copy, scale=0.0625)
+            else:
+                nc.vector.tensor_scalar(s_win[t][:, :V], acc[:], 0.0625, None, ALU.mult)
         for t in range(PACK):
             s_n8 = sbuf("s_n8_%d" % t, [P, V], F32)
             scaled = sbuf("scaled%d" % t, [P, V], F32)
             nc.scalar.activation(s_n8[:], s_win[t][:].indirect(lists["n8"][:]), ACT.Copy)
-            nc.vector.tensor_tensor(scaled[:], s_n8[:], tab_n6[t][:], ALU.mult)
-            nc.vector.tensor_tensor(result[:, t, :], scaled[:], tab_n7[t][:], ALU.add)
+            nc.vector.tensor_tensor(scaled[:], s_n8[:], tab_at["n6", t], ALU.mult)
+            nc.vector.tensor_tensor(result[:, t, :], scaled[:], tab_at["n7", t], ALU.add)
             nc.sync.dma_start(out_rows[:, t, :], result[:, t, :])
 
         out_grouped = sbuf("out_grouped", [P, V, PACK], BF16)

@@ -21,7 +21,6 @@ ACT = mybir.ActivationFunctionType
 
 Y_WINDOW = S + 16
 Q_WINDOW = 2 * V
-LN_FLOOR = 2.0 ** -60
 
 
 def tile_picked_twknormbwsumkinda_none_po_kernel(
@@ -45,9 +44,9 @@ def tile_picked_twknormbwsumkinda_none_po_kernel(
             lists[name] = sbuf("list_" + name, list(dram.shape), U16)
             nc.sync.dma_start(lists[name][:], dram)
 
-        def load_scales(queue, tile, dram):
+        def load_scales(tile, dram):
             for q in range(4):
-                queue.dma_start(tile[32 * q : 32 * q + 4, :].bitcast(I32), dram[0, 4 * q : 4 * q + 4, :].bitcast(I32))
+                nc.sync.dma_start(tile[32 * q : 32 * q + 4, :].bitcast(I32), dram[0, 4 * q : 4 * q + 4, :].bitcast(I32))
 
         def load_fp4(name, dram):
             tile = sbuf(name, [P, 2 * H], U8)
@@ -58,49 +57,55 @@ def tile_picked_twknormbwsumkinda_none_po_kernel(
         w1s = sbuf("w1s", [P, H], U8)
         w2s = sbuf("w2s", [P, H], U8)
         w3s_raw = sbuf("w3s_raw", [P, H], U8)
-        half = sbuf("half", [P, 1], F32)
+        zero = sbuf("zero", [P, 1], F32, tag="after_sigmoid")
         nc.gpsimd.memset(xs[:].bitcast(I32), 0)
         nc.gpsimd.memset(w2s[:].bitcast(I32), 0)
-        nc.vector.memset(half[:], 0.5)
+        nc.vector.memset(zero[:], 0.0)
+        ga_rows = sbuf("ga_rows", [P, P], F32)
+        nc.vector.memset(ga_rows[:], 0.0)
         nc.vector.memset(w1s[:].bitcast(I32), 0)
         nc.vector.memset(w3s_raw[:].bitcast(I32), 0)
 
         tab_rows = tab.rearrange("(p t) j -> t p j", t=PACK)
         tabs = [sbuf("tab%d" % t, [P, J], F32) for t in range(PACK)]
         xw = sbuf("xw", [P, T], U32)
-        ga_sb = sbuf("ga_sb", [P, PACK], F32)
         gb_sb = sbuf("gb_sb", [P, PACK], F32)
 
-        nc.scalar.dma_start(xw[:].bitcast(I32), x_words[0].rearrange("p n t -> p (n t)").bitcast(I32))
+        nc.gpsimd.dma_start(ga_rows[:4, :], ga.rearrange("(f p) o -> f (p o)", p=P))
+        x_rows = x_words[0].rearrange("p n t -> p (n t)").bitcast(I32)
+        nc.sync.dma_start(xw[:, : T // 2].bitcast(I32), x_rows[:, : T // 2])
+        load_scales(xs, x_scales)
         load_list("two", two)
-        load_scales(nc.sync, xs, x_scales)
-        load_scales(nc.gpsimd, w2s, w2_scales)
+        nc.sync.dma_start(xw[:, T // 2 :].bitcast(I32), x_rows[:, T // 2 :])
         load_list("offs", offs)
         w2w = load_fp4("w2w", w2_words)
+        load_scales(w2s, w2_scales)
         w1w = load_fp4("w1w", w1_words)
-        load_scales(nc.sync, w1s, w1_scales)
-        with nc.allow_non_contiguous_dma(reason="one weight a partition and feature tile"):
-            nc.sync.dma_start(ga_sb[:], ga.rearrange("(f p) o -> p (f o)", p=P))
-        nc.sync.dma_start(tabs[0][:], tab_rows[0])
+        w3w_raw = load_fp4("w3w_raw", w3_words)
+        load_list("three", three)
+        load_scales(w1s, w1_scales)
+        load_list("n1", n1)
+        load_scales(w3s_raw, w3_scales)
+        for name, dram in (("n2", n2), ("n5", n5), ("n3", n3), ("n4", n4)):
+            load_list(name, dram)
+        nc.sync.dma_start(tabs[2][:], tab_rows[2])
+        nc.sync.dma_start(tabs[3][:], tab_rows[3])
         load_list("n6", n6)
         load_list("n7", n7)
-        w3w_raw = load_fp4("w3w_raw", w3_words)
-        load_scales(nc.sync, w3s_raw, w3_scales)
-        load_list("n2", n2)
-        load_list("n1", n1)
-        load_list("three", three)
         nc.sync.dma_start(gb_sb[:], gb.rearrange("(p t) o -> p (t o)", t=PACK))
-        for name, dram in (("n3", n3), ("n4", n4), ("n5", n5), ("n8", n8)):
-            load_list(name, dram)
-        for t in range(1, PACK):
-            nc.sync.dma_start(tabs[t][:], tab_rows[t])
+        nc.sync.dma_start(tabs[0][:], tab_rows[0])
+        nc.sync.dma_start(tabs[1][:], tab_rows[1])
+        load_list("n8", n8)
 
-        ln_half = sbuf("ln_half", [P, 1], F32)
-        nc.scalar.activation(ln_half[:], half[:], ACT.Ln)
+        half = sbuf("half", [P, 1], F32)
+        nc.scalar.activation(half[:], zero[:], ACT.Sigmoid)
         ident = sbuf("ident", [P, P], F32)
         make_identity(nc, ident[:])
-        ln_floor = sbuf("ln_floor", [P, 1], F32, tag="after_ln")
-        nc.vector.memset(ln_floor[:], LN_FLOOR)
+        ga_turned = bank("ga_turned", 7, [P, P])
+        nc.tensor.transpose(ga_turned[:], ga_rows[:], ident[:])
+        ga_col = [sbuf("ga_col%d" % f, [P, 1], F32) for f in range(4)]
+        for f in range(4):
+            nc.scalar.copy(ga_col[f][:], ga_turned[:, f : f + 1])
 
         def window(name, used, width):
             tile = sbuf(name, [P, width], F32)
@@ -110,17 +115,14 @@ def tile_picked_twknormbwsumkinda_none_po_kernel(
         d_abs = [sbuf("d_abs%d" % f, [P, S], F32) for f in range(4)]
         y_win = [window("y_win%d" % f, S, Y_WINDOW) for f in range(4)]
         b_win = [window("b_win%d" % t, V, Q_WINDOW) for t in range(PACK)]
+        sig_win = [window("sig_win%d" % t, V, Q_WINDOW) for t in range(PACK)]
         s_win = b_win
 
-        w3w = sbuf("w3w", [P, 2 * H], U8)
-        w3s = sbuf("w3s", [P, H], U8)
-
-        def pick(name, width):
-            words = sbuf("words_" + name, [P, width], U32)
-            scales = sbuf("scales_" + name, [P, width], U8)
-            nc.vector.tensor_copy(scales[:], xs[:].indirect(lists[name][:]))
-            nc.vector.tensor_copy(words[:], xw[:].indirect(lists[name][:]))
-            return words, scales
+        def pick(source, dtype, name, width, slot=""):
+            size = 4 if dtype is U32 else 1
+            picked = sbuf("%s_%d" % (name, size), [P, width], dtype, tag=slot)
+            nc.vector.tensor_copy(picked[:], source[:].indirect(lists[name][:]))
+            return picked
 
         def project(out, w_words, w_scales, tile, picked):
             nc.tensor.matmul_mx(
@@ -148,127 +150,133 @@ def tile_picked_twknormbwsumkinda_none_po_kernel(
             else:
                 nc.vector.tensor_copy(out, looked_up)
 
-        x_two = pick("two", S)
+        scales_two = pick(xs, U8, "two", S)
+        x_two = (pick(xw, U32, "two", S), scales_two)
+        scales_offs = pick(xs, U8, "offs", S)
+        x_offs = (pick(xw, U32, "offs", S), scales_offs)
+        scales_three = pick(xs, U8, "three", V)
         for f in range(4):
             acc = bank("d_acc%d" % f, f, [P, S])
             project(acc[:], w2w, w2s, f, x_two)
             nc.scalar.activation(d_abs[f][:], acc[:], ACT.Abs)
-        x_offs = pick("offs", S)
-        y_acc = []
-        for f in range(4):
-            y_acc.append(bank("y_acc%d" % f, 4 + f, [P, S]))
-            project(y_acc[f][:], w1w, w1s, f, x_offs)
-
-        tab_at = {}
-        for name in ("n6", "n7"):
-            tab_at[name, 0] = sbuf("tab_%s_0" % name, [P, V], F32)[:]
-            tab_gather(nc.scalar, name, 0, tab_at[name, 0])
-
-        ln_sum = sbuf("ln_sum", [P, 4, S], F32)
-        sums = {}
-        diff = {}
-
-        def denominator(f):
-            d_n2 = sbuf("d_n2_%d" % f, [P, S], F32)
-            for i in range(2):
-                nc.vector.tensor_copy(d_n2[:, 256 * i : 256 * (i + 1)], d_abs[f][:].indirect(lists["n2"][:, 16 * i : 16 * (i + 1)]))
-            sums[f] = turn_and_add("sum_t%d" % f, f, d_abs[f], d_n2)
-
-        def logarithm(f):
-            nc.scalar.activation(ln_sum[:, f, :], sums[f][:].rearrange("p u c -> p (u c)"), ACT.Ln, bias=ln_floor[:])
-
-        def y_out(f):
-            nc.vector.tensor_scalar(y_win[f][:, :S], y_acc[f][:], ga_sb[:, f : f + 1], 2.0, ALU.mult, ALU.mult)
-
-        def numerator(f):
-            y_n1 = sbuf("y_n1_%d" % f, [P, S], F32)
-            nc.scalar.activation(y_n1[:], y_win[f][:].indirect(lists["n1"][:]), ACT.Copy, scale=-1.0)
-            diff[f] = turn_and_add("diff_t%d" % f, 4 + f, y_win[f], y_n1)
-
-        denominator(0)
-        y_out(0)
-        y_out(1)
-        numerator(0)
-        logarithm(0)
-        denominator(1)
-        y_out(2)
-        y_out(3)
-        numerator(1)
-        logarithm(1)
-        denominator(2)
-        numerator(2)
-        denominator(3)
-        logarithm(2)
-        numerator(3)
-        logarithm(3)
-
-        nc.vector.tensor_copy(
-            w3w[:].rearrange("p (t m b) -> p t m b", t=PACK, b=2),
-            w3w_raw[:].rearrange("p (m t b) -> p t m b", t=PACK, b=2),
+        w3w = sbuf("w3w", [P, 2 * H], U8)
+        nc.scalar.copy(
+            w3w[:].bitcast(U16).rearrange("p (t m) -> p t m", t=PACK),
+            w3w_raw[:].bitcast(U16).rearrange("p (m t) -> p t m", t=PACK),
         )
+        y_n1 = []
+        for f in range(4):
+            acc = bank("y_acc%d" % f, 4 + f, [P, S])
+            project(acc[:], w1w, w1s, f, x_offs)
+            nc.vector.tensor_scalar(y_win[f][:, :S], acc[:], ga_col[f][:], None, ALU.mult)
+            y_n1.append(sbuf("y_n1_%d" % f, [P, S], F32))
+            nc.scalar.activation(y_n1[f][:], y_win[f][:].indirect(lists["n1"][:]), ACT.Copy, scale=-1.0)
+        x_three = (pick(xw, U32, "three", V, "ga_col1"), scales_three)
+        w3s = sbuf("w3s", [P, H], U8, tag="ga_col2")
         nc.vector.tensor_copy(
             w3s[:].rearrange("p (t m) -> p t m", t=PACK),
             w3s_raw[:].rearrange("p (m t) -> p t m", t=PACK),
         )
-        x_three = pick("three", V)
-        for t in range(2, PACK):
-            for name in ("n6", "n7"):
-                tab_at[name, t] = sbuf("tab_%s_%d" % (name, t), [P, V], F32)[:]
         b_acc = []
         for pair in range(2):
-            b_acc.append(bank("b_acc%d" % pair, pair, [P, 2, V]))
+            b_acc.append(bank("b_acc%d" % pair, 6 + pair, [P, 2, V]))
             for i in range(2):
                 project(b_acc[pair][:, i, :], w3w, w3s, 2 * pair + i, x_three)
         for t in range(PACK):
+            nc.scalar.activation(sig_win[t][:, :V], b_acc[t // 2][:, t % 2, :], ACT.Sigmoid, bias=zero[:])
+
+        sums = {}
+        diff = {}
+
+        def denominator(f):
+            d_n2 = sbuf("d_n2_%d" % f, [P, S], F32, tag=("ga_col3", "w3s_raw", "w3w", "three_1")[f])
+            for i in range(2):
+                nc.vector.tensor_copy(d_n2[:, 256 * i : 256 * (i + 1)], d_abs[f][:].indirect(lists["n2"][:, 16 * i : 16 * (i + 1)]))
+            sums[f] = turn_and_add("sum_t%d" % f, f, d_abs[f], d_n2)
+
+        def numerator(f):
+            diff[f] = turn_and_add("diff_t%d" % f, 4 + f, y_win[f], y_n1[f])
+
+        numerator(0)
+        denominator(0)
+        denominator(1)
+        numerator(1)
+        denominator(2)
+        denominator(3)
+        for t in range(PACK):
             nc.vector.tensor_copy(b_win[t][:, :V], b_acc[t // 2][:, t % 2, :])
+        numerator(2)
+        numerator(3)
+        tab_at = {}
         for t in range(2, PACK):
-            for name in ("n6", "n7"):
+            both = sbuf("tab_at%d" % t, [P, 2, V], F32, tag="d_abs%d" % t)
+            for i, name in enumerate(("n6", "n7")):
+                tab_at[name, t] = both[:, i, :]
                 tab_gather(nc.vector, name, t, tab_at[name, t])
-
-        late = sbuf("late", [P, 4 * S + (4 * PACK + 2) * V], F32, tag="after_ln")
-
-        def late_cols(i):
-            return late[:, 4 * S + V * i : 4 * S + V * (i + 1)]
-
+        root = sbuf("root", [P, 4, S], F32, tag="after_sigmoid")
+        rec = sbuf("rec", [P, 4, S], F32)
         z_t = sbuf("z_t", [P, 4, H], BF16)
-        for f in range(4):
-            rec = late[:, S * f : S * (f + 1)]
-            nc.scalar.activation(rec, ln_sum[:, f, :], ACT.Sigmoid, bias=ln_half[:], scale=-1.0)
-            nc.vector.tensor_tensor(z_t[:, :, P * f : P * (f + 1)], diff[f][:], rec.rearrange("p (u c) -> p u c", u=4), ALU.mult)
+        z2 = sbuf("z2", [P, PACK, V], F32)
 
+        def inverse_root(f):
+            nc.scalar.activation(root[:, f, :], sums[f][:].rearrange("p u c -> p (u c)"), ACT.Abs_reciprocal_sqrt, bias=half[:])
+
+        def square(f):
+            if f < 2:
+                nc.vector.tensor_tensor(rec[:, f, :], root[:, f, :], root[:, f, :], ALU.mult)
+            else:
+                nc.scalar.activation(rec[:, f, :], root[:, f, :], ACT.Square)
+
+        def ratio(f):
+            nc.vector.tensor_tensor(z_t[:, :, P * f : P * (f + 1)], diff[f][:], rec[:, f, :].rearrange("p (u c) -> p u c", u=4), ALU.mult)
+
+        def gated(t):
+            got = sbuf("gated%d" % t, [P, 5, V], F32)
+            sig_n5, b_n3, b_n4, left, right = [got[:, i, :] for i in range(5)]
+            nc.scalar.activation(sig_n5, sig_win[t][:].indirect(lists["n5"][:]), ACT.Copy)
+            nc.scalar.activation(b_n3, b_win[t][:].indirect(lists["n3"][:]), ACT.Copy)
+            nc.scalar.activation(b_n4, b_win[t][:].indirect(lists["n4"][:]), ACT.Copy)
+            nc.vector.scalar_tensor_tensor(left, b_n3, gb_sb[:, t : t + 1], sig_win[t][:, :V], ALU.mult, ALU.mult)
+            nc.vector.scalar_tensor_tensor(right, b_n4, gb_sb[:, t : t + 1], sig_n5, ALU.mult, ALU.mult)
+            nc.vector.tensor_tensor(z2[:, t, :], left, right, ALU.add)
+
+        inverse_root(0)
+        inverse_root(1)
+        square(0)
+        square(1)
+        ratio(0)
+        ratio(1)
+        gated(0)
+        inverse_root(2)
+        inverse_root(3)
+        square(2)
+        square(3)
+        ratio(2)
+        ratio(3)
         z_grouped = sbuf("z_grouped", [P, PACK * S], BF16)
         z_grouped_words = z_grouped[:].bitcast(F32).rearrange("p (t u m h) -> p u t m h", t=PACK, u=4, h=2)
         z_back = []
         for pair in range(2):
-            z_back.append(bank("z_back%d" % pair, 2 + pair, [P, 2, 2, P]))
+            z_back.append(bank("z_back%d" % pair, pair, [P, 2, 2, P]))
             for i in range(2):
                 words = z_t[:, 2 * pair + i, :].bitcast(F32)
                 for h in range(2):
                     nc.tensor.transpose(z_back[pair][:, i, h, :], words[:, h::2], ident[:])
-
+        gated(1)
+        for pair in range(2):
+            nc.vector.tensor_copy(
+                z_grouped_words[:, 2 * pair : 2 * pair + 2], z_back[pair][:].rearrange("p i h (m t) -> p i t m h", t=PACK)
+            )
+        gated(2)
         z_words = sbuf("z_words", [P, S], U32)
         z_scales = sbuf("z_scales", [P, S], U8)
-        z2 = sbuf("z2", [P, PACK, V], F32)
-        for t in range(PACK):
-            b_n3, sig_b, b_n4, sig_n5 = [late_cols(4 * t + i) for i in range(4)]
-            left = sbuf("left%d" % t, [P, V], F32)
-            right = sbuf("right%d" % t, [P, V], F32)
-            nc.scalar.activation(b_n3, b_win[t][:].indirect(lists["n3"][:]), ACT.Copy)
-            nc.scalar.activation(sig_b, b_win[t][:, :V], ACT.Sigmoid)
-            nc.scalar.activation(b_n4, b_win[t][:].indirect(lists["n4"][:]), ACT.Copy)
-            nc.scalar.activation(sig_n5, b_win[t][:].indirect(lists["n5"][:]), ACT.Sigmoid)
-            nc.vector.scalar_tensor_tensor(left[:], b_n3, gb_sb[:, t : t + 1], sig_b, ALU.mult, ALU.mult)
-            if t < 2:
-                nc.vector.tensor_copy(
-                    z_grouped_words[:, 2 * t : 2 * t + 2], z_back[t][:].rearrange("p i h (m t) -> p i t m h", t=PACK)
-                )
-            if t == 2:
-                nc.vector.quantize_mx(z_words[:].bitcast(FP8X4), z_scales[:], z_grouped[:])
-            nc.vector.scalar_tensor_tensor(right[:], b_n4, gb_sb[:, t : t + 1], sig_n5, ALU.mult, ALU.mult)
-            nc.vector.tensor_tensor(z2[:, t, :], left[:], right[:], ALU.add)
-        for i, name in enumerate(("n6", "n7")):
-            tab_at[name, 1] = late_cols(4 * PACK + i)
-            tab_gather(nc.scalar, name, 1, tab_at[name, 1])
+        nc.vector.quantize_mx(z_words[:].bitcast(FP8X4), z_scales[:], z_grouped[:])
+        gated(3)
+        for t in range(2):
+            both = sbuf("tab_at%d" % t, [P, 2, V], F32, tag="sig_win%d" % t)
+            for i, name in enumerate(("n6", "n7")):
+                tab_at[name, t] = both[:, i, :]
+                tab_gather(nc.scalar, name, t, tab_at[name, t])
         z2_grouped = sbuf("z2_grouped", [P, V, PACK], BF16)
         nc.vector.tensor_copy(
             z2_grouped[:].rearrange("p (c i) t -> p c t i", i=4), z2[:].rearrange("p t (c i) -> p c t i", i=4)

from contextlib import ExitStack

import concourse.mybir as mybir
from concourse.masks import make_identity

K, T, S, V, H, J = 512, 2048, 512, 256, 512, 512
P = 128
PACK = 4
FLOPS = 2 * K * H * (S + S + V) + 2 * H * S * V

F32 = mybir.dt.float32
BF16 = mybir.dt.bfloat16
I32 = mybir.dt.int32
U32 = mybir.dt.uint32
U16 = mybir.dt.uint16
U8 = mybir.dt.uint8
FP8X4 = mybir.dt.float8_e4m3fn_x4
FP4X4 = mybir.dt.float4_e2m1fn_x4
ALU = mybir.AluOpType
ACT = mybir.ActivationFunctionType

Y_WINDOW = S + 16
Q_WINDOW = 2 * V


def tile_picked_twknormbwsumkinda_none_po_kernel(
    tc, x_words, x_scales, w1_words, w1_scales, w2_words, w2_scales, w3_words, w3_scales,
    ga, gb, tab, offs, two, n1, n2, three, n3, n4, n5, n6, n7, n8, out_0, out_1, out_2,
):
    nc = tc.nc
    with ExitStack() as ctx:
        keep = ctx.enter_context(tc.tile_pool(name="keep", bufs=1))
        psum = ctx.enter_context(tc.psum_pool(name="psum", bufs=1))

        def sbuf(name, shape, dtype, tag=""):
            return keep.tile(shape, dtype, name=name, tag=tag or name, align_bytes=64)

        def bank(name, number, shape):
            return psum.tile(shape, F32, name=name, tag="bank%d" % number)

        lists = {}

        def load_list(name, dram):
            lists[name] = sbuf("list_" + name, list(dram.shape), U16)
            nc.sync.dma_start(lists[name][:], dram)

        def load_scales(tile, dram):
            for q in range(4):
                nc.sync.dma_start(tile[32 * q : 32 * q + 4, :].bitcast(I32), dram[0, 4 * q : 4 * q + 4, :].bitcast(I32))

        def load_fp4(name, dram):
            tile = sbuf(name, [P, 2 * H], U8)
            nc.sync.dma_start(tile[:].bitcast(I32), dram[0].bitcast(I32))
            return tile

        xs = sbuf("xs", [P, T], U8)
        w1s = sbuf("w1s", [P, H], U8)
        w2s = sbuf("w2s", [P, H], U8)
        w3s_raw = sbuf("w3s_raw", [P, H], U8)
        zero = sbuf("zero", [P, 1], F32, tag="after_sigmoid")
        nc.gpsimd.memset(xs[:].bitcast(I32), 0)
        nc.gpsimd.memset(w2s[:].bitcast(I32), 0)
        nc.vector.memset(zero[:], 0.0)
        ga_rows = sbuf("ga_rows", [P, P], F32)
        nc.vector.memset(ga_rows[:], 0.0)
        nc.vector.memset(w1s[:].bitcast(I32), 0)
        nc.vector.memset(w3s_raw[:].bitcast(I32), 0)

        tab_rows = tab.rearrange("(p t) j -> t p j", t=PACK)
        tabs = [sbuf("tab%d" % t, [P, J], F32) for t in range(PACK)]
        xw = sbuf("xw", [P, T], U32)
        gb_sb = sbuf("gb_sb", [P, PACK], F32)

        nc.gpsimd.dma_start(ga_rows[:4, :], ga.rearrange("(f p) o -> f (p o)", p=P))
        x_rows = x_words[0].rearrange("p n t -> p (n t)").bitcast(I32)
        nc.sync.dma_start(xw[:, : T // 2].bitcast(I32), x_rows[:, : T // 2])
        load_scales(xs, x_scales)
        load_list("two", two)
        nc.sync.dma_start(xw[:, T // 2 :].bitcast(I32), x_rows[:, T // 2 :])
        load_list("offs", offs)
        w2w = load_fp4("w2w", w2_words)
        load_scales(w2s, w2_scales)
        w1w = load_fp4("w1w", w1_words)
        w3w_raw = load_fp4("w3w_raw", w3_words)
        load_list("three", three)
        load_scales(w1s, w1_scales)
        load_list("n1", n1)
        load_scales(w3s_raw, w3_scales)
        for name, dram in (("n2", n2), ("n5", n5), ("n3", n3), ("n4", n4)):
            load_list(name, dram)
        nc.sync.dma_start(tabs[2][:], tab_rows[2])
        nc.sync.dma_start(tabs[3][:], tab_rows[3])
        load_list("n6", n6)
        load_list("n7", n7)
        nc.sync.dma_start(gb_sb[:], gb.rearrange("(p t) o -> p (t o)", t=PACK))
        nc.sync.dma_start(tabs[0][:], tab_rows[0])
        nc.sync.dma_start(tabs[1][:], tab_rows[1])
        load_list("n8", n8)

        half = sbuf("half", [P, 1], F32)
        nc.scalar.activation(half[:], zero[:], ACT.Sigmoid)
        ident = sbuf("ident", [P, P], F32)
        make_identity(nc, ident[:])
        ga_turned = bank("ga_turned", 7, [P, P])
        nc.tensor.transpose(ga_turned[:], ga_rows[:], ident[:])
        ga_col = [sbuf("ga_col%d" % f, [P, 1], F32) for f in range(4)]
        for f in range(4):
            nc.scalar.copy(ga_col[f][:], ga_turned[:, f : f + 1])

        def window(name, used, width):
            tile = sbuf(name, [P, width], F32)
            nc.vector.memset(tile[:, used:], 0.0)
            return tile

        d_abs = [sbuf("d_abs%d" % f, [P, S], F32) for f in range(4)]
        y_win = [window("y_win%d" % f, S, Y_WINDOW) for f in range(4)]
        b_win = [window("b_win%d" % t, V, Q_WINDOW) for t in range(PACK)]
        sig_win = [window("sig_win%d" % t, V, Q_WINDOW) for t in range(PACK)]
        s_win = b_win

        def pick(source, dtype, name, width, slot=""):
            size = 4 if dtype is U32 else 1
            picked = sbuf("%s_%d" % (name, size), [P, width], dtype, tag=slot)
            nc.vector.tensor_copy(picked[:], source[:].indirect(lists[name][:]))
            return picked

        def project(out, w_words, w_scales, tile, picked):
            nc.tensor.matmul_mx(
                out,
                lhsT=w_words[:, 2 * P * tile : 2 * P * (tile + 1)].bitcast(FP4X4),
                lhsT_scale=w_scales[:, P * tile : P * (tile + 1)],
                rhs=picked[0][:].bitcast(FP8X4),
                rhs_scale=picked[1][:],
                start=True,
                stop=True,
            )

        def turn_and_add(name, number, first, second):
            acc = bank(name, number, [P, 4, P])
            for u in range(4):
                cols = slice(P * u, P * (u + 1))
                nc.tensor.matmul(acc[:, u, :], lhsT=first[:, cols], rhs=ident[:], is_transpose=True, start=True, stop=False)
                nc.tensor.matmul(acc[:, u, :], lhsT=second[:, cols], rhs=ident[:], is_transpose=True, start=False, stop=True)
            return acc

        def tab_gather(engine, name, t, out):
            looked_up = tabs[t][:].indirect(lists[name][:])
            if engine is nc.scalar:
                nc.scalar.activation(out, looked_up, ACT.Copy)
            else:
                nc.vector.tensor_copy(out, looked_up)

        scales_two = pick(xs, U8, "two", S)
        x_two = (pick(xw, U32, "two", S), scales_two)
        scales_offs = pick(xs, U8, "offs", S)
        x_offs = (pick(xw, U32, "offs", S), scales_offs)
        scales_three = pick(xs, U8, "three", V)
        for f in range(4):
            acc = bank("d_acc%d" % f, f, [P, S])
            project(acc[:], w2w, w2s, f, x_two)
            nc.scalar.activation(d_abs[f][:], acc[:], ACT.Abs)
        w3w = sbuf("w3w", [P, 2 * H], U8)
        nc.scalar.copy(
            w3w[:].bitcast(U16).rearrange("p (t m) -> p t m", t=PACK),
            w3w_raw[:].bitcast(U16).rearrange("p (m t) -> p t m", t=PACK),
        )
        y_n1 = []
        for f in range(4):
            acc = bank("y_acc%d" % f, 4 + f, [P, S])
            project(acc[:], w1w, w1s, f, x_offs)
            nc.vector.tensor_scalar(y_win[f][:, :S], acc[:], ga_col[f][:], None, ALU.mult)
            y_n1.append(sbuf("y_n1_%d" % f, [P, S], F32))
            nc.scalar.activation(y_n1[f][:], y_win[f][:].indirect(lists["n1"][:]), ACT.Copy, scale=-1.0)
        x_three = (pick(xw, U32, "three", V, "ga_col1"), scales_three)
        w3s = sbuf("w3s", [P, H], U8, tag="ga_col2")
        nc.vector.tensor_copy(
            w3s[:].rearrange("p (t m) -> p t m", t=PACK),
            w3s_raw[:].rearrange("p (m t) -> p t m", t=PACK),
        )
        b_acc = []
        for pair in range(2):
            b_acc.append(bank("b_acc%d" % pair, 6 + pair, [P, 2, V]))
            for i in range(2):
                project(b_acc[pair][:, i, :], w3w, w3s, 2 * pair + i, x_three)
        for t in range(PACK):
            nc.scalar.activation(sig_win[t][:, :V], b_acc[t // 2][:, t % 2, :], ACT.Sigmoid, bias=zero[:])

        sums = {}
        diff = {}

        def denominator(f):
            d_n2 = sbuf("d_n2_%d" % f, [P, S], F32, tag=("ga_col3", "w3s_raw", "w3w", "three_1")[f])
            for i in range(2):
                nc.vector.tensor_copy(d_n2[:, 256 * i : 256 * (i + 1)], d_abs[f][:].indirect(lists["n2"][:, 16 * i : 16 * (i + 1)]))
            sums[f] = turn_and_add("sum_t%d" % f, f, d_abs[f], d_n2)

        def numerator(f):
            diff[f] = turn_and_add("diff_t%d" % f, 4 + f, y_win[f], y_n1[f])

        numerator(0)
        denominator(0)
        denominator(1)
        numerator(1)
        denominator(2)
        denominator(3)
        for t in range(PACK):
            nc.vector.tensor_copy(b_win[t][:, :V], b_acc[t // 2][:, t % 2, :])
        numerator(2)
        numerator(3)
        tab_at = {}
        for t in range(2, PACK):
            both = sbuf("tab_at%d" % t, [P, 2, V], F32, tag="d_abs%d" % t)
            for i, name in enumerate(("n6", "n7")):
                tab_at[name, t] = both[:, i, :]
                tab_gather(nc.vector, name, t, tab_at[name, t])
        root = sbuf("root", [P, 4, S], F32, tag="after_sigmoid")
        rec = sbuf("rec", [P, 4, S], F32)
        z_t = sbuf("z_t", [P, 4, H], BF16)
        z2 = sbuf("z2", [P, PACK, V], F32)

        def inverse_root(f):
            nc.scalar.activation(root[:, f, :], sums[f][:].rearrange("p u c -> p (u c)"), ACT.Abs_reciprocal_sqrt, bias=half[:])

        def square(f):
            if f < 2:
                nc.vector.tensor_tensor(rec[:, f, :], root[:, f, :], root[:, f, :], ALU.mult)
            else:
                nc.scalar.activation(rec[:, f, :], root[:, f, :], ACT.Square)

        def ratio(f):
            nc.vector.tensor_tensor(z_t[:, :, P * f : P * (f + 1)], diff[f][:], rec[:, f, :].rearrange("p (u c) -> p u c", u=4), ALU.mult)

        def gated(t):
            got = sbuf("gated%d" % t, [P, 5, V], F32)
            sig_n5, b_n3, b_n4, left, right = [got[:, i, :] for i in range(5)]
            nc.scalar.activation(sig_n5, sig_win[t][:].indirect(lists["n5"][:]), ACT.Copy)
            nc.scalar.activation(b_n3, b_win[t][:].indirect(lists["n3"][:]), ACT.Copy)
            nc.scalar.activation(b_n4, b_win[t][:].indirect(lists["n4"][:]), ACT.Copy)
            nc.vector.scalar_tensor_tensor(left, b_n3, gb_sb[:, t : t + 1], sig_win[t][:, :V], ALU.mult, ALU.mult)
            nc.vector.scalar_tensor_tensor(right, b_n4, gb_sb[:, t : t + 1], sig_n5, ALU.mult, ALU.mult)
            nc.vector.tensor_tensor(z2[:, t, :], left, right, ALU.add)

        inverse_root(0)
        inverse_root(1)
        square(0)
        square(1)
        ratio(0)
        ratio(1)
        gated(0)
        inverse_root(2)
        inverse_root(3)
        square(2)
        square(3)
        ratio(2)
        ratio(3)
        z_grouped = sbuf("z_grouped", [P, PACK * S], BF16)
        z_grouped_words = z_grouped[:].bitcast(F32).rearrange("p (t u m h) -> p u t m h", t=PACK, u=4, h=2)
        z_back = []
        for pair in range(2):
            z_back.append(bank("z_back%d" % pair, pair, [P, 2, 2, P]))
            for i in range(2):
                words = z_t[:, 2 * pair + i, :].bitcast(F32)
                for h in range(2):
                    nc.tensor.transpose(z_back[pair][:, i, h, :], words[:, h::2], ident[:])
        gated(1)
        for pair in range(2):
            nc.vector.tensor_copy(
                z_grouped_words[:, 2 * pair : 2 * pair + 2], z_back[pair][:].rearrange("p i h (m t) -> p i t m h", t=PACK)
            )
        gated(2)
        z_words = sbuf("z_words", [P, S], U32)
        z_scales = sbuf("z_scales", [P, S], U8)
        nc.vector.quantize_mx(z_words[:].bitcast(FP8X4), z_scales[:], z_grouped[:])
        gated(3)
        for t in range(2):
            both = sbuf("tab_at%d" % t, [P, 2, V], F32, tag="sig_win%d" % t)
            for i, name in enumerate(("n6", "n7")):
                tab_at[name, t] = both[:, i, :]
                tab_gather(nc.scalar, name, t, tab_at[name, t])
        z2_grouped = sbuf("z2_grouped", [P, V, PACK], BF16)
        nc.vector.tensor_copy(
            z2_grouped[:].rearrange("p (c i) t -> p c t i", i=4), z2[:].rearrange("p t (c i) -> p c t i", i=4)
        )
        z2_words = sbuf("z2_words", [P, V], U32)
        z2_scales = sbuf("z2_scales", [P, V], U8)
        nc.vector.quantize_mx(z2_words[:].bitcast(FP8X4), z2_scales[:], z2_grouped[:].rearrange("p c t -> p (c t)"))

        result = sbuf("result", [P, PACK, V], F32)
        out_rows = out_0.rearrange("(p t) v -> p t v", t=PACK)
        for t in range(PACK):
            acc = bank("s_acc%d" % t, 4 + t, [P, V])
            cols = slice(P * t, P * (t + 1))
            nc.tensor.matmul_mx(
                acc[:],
                lhsT=z_words[:, cols].bitcast(FP8X4),
                lhsT_scale=z_scales[:, cols],
                rhs=z2_words[:].bitcast(FP8X4),
                rhs_scale=z2_scales[:],
                start=True,
                stop=True,
            )
            if t == 0:
                nc.scalar.activation(s_win[t][:, :V], acc[:], ACT.Copy, scale=0.0625)
            else:
                nc.vector.tensor_scalar(s_win[t][:, :V], acc[:], 0.0625, None, ALU.mult)
        for t in range(PACK):
            s_n8 = sbuf("s_n8_%d" % t, [P, V], F32)
            scaled = sbuf("scaled%d" % t, [P, V], F32)
            nc.scalar.activation(s_n8[:], s_win[t][:].indirect(lists["n8"][:]), ACT.Copy)
            nc.vector.tensor_tensor(scaled[:], s_n8[:], tab_at["n6", t], ALU.mult)
            nc.vector.tensor_tensor(result[:, t, :], scaled[:], tab_at["n7", t], ALU.add)
            nc.sync.dma_start(out_rows[:, t, :], result[:, t, :])

        out_grouped = sbuf("out_grouped", [P, V, PACK], BF16)
        nc.vector.tensor_copy(
            out_grouped[:].rearrange("p (c i) t -> p c t i", i=4), result[:].rearrange("p t (c i) -> p c t i", i=4)
        )
        out_words = sbuf("out_words", [P, V], U32)
        out_scales = sbuf("out_scales", [P, V], U8)
        nc.vector.quantize_mx(out_words[:].bitcast(FP8X4), out_scales[:], out_grouped[:].rearrange("p c t -> p (c t)"))
        nc.sync.dma_start(out_1[0].rearrange("p n t -> p (n t)").bitcast(I32), out_words[:].bitcast(I32))
        for q in range(4):
            nc.sync.dma_start(out_2[0, 4 * q : 4 * q + 4, :].bitcast(I32), out_scales[32 * q : 32 * q + 4, :].bitcast(I32))
